import numpy as np
import ml_dtypes


def mxq(x, axis, fmt="e4m3"):
    dtype, down = {"e4m3": (ml_dtypes.float8_e4m3fn, 7), "e5m2": (ml_dtypes.float8_e5m2, 14)}[fmt]
    v = np.moveaxis(np.asarray(x, np.float32).astype(ml_dtypes.bfloat16).astype(np.float64), axis, -1)
    blocks = v.reshape(v.shape[:-1] + (-1, 32))
    amax = np.abs(blocks).max(-1, keepdims=True)
    byte = np.maximum(np.where(amax > 0, np.frexp(amax)[1] - 1 + 127, 0) - down, 1)
    scale = np.exp2(byte - 127.0)
    codes = (blocks / scale).astype(np.float32).astype(dtype).astype(np.float64)
    return np.moveaxis((codes * scale).reshape(v.shape), -1, axis)


WIDE = False


def mx_kscale(k):
    if not WIDE:
        return np.ones(k)
    levels = np.array([10, -10, 5, -5, 0])
    if k % 512:
        return np.exp2(np.random.permutation(np.resize(levels, k // 32))).repeat(32)
    a = np.empty((k // 512, 16))
    for p in range(k // 512):
        a[p, :8] = np.random.permutation(np.resize(levels, 8))
        for g in range(8):
            far = levels[np.abs(levels - a[p, g]) >= 10]
            a[p, g + 8] = far[np.random.randint(len(far))]
    return np.exp2(a.ravel()).repeat(32)


def f64(x):
    return np.asarray(x).astype(np.float64)


def striped(idx):
    return np.tile(np.asarray(idx).reshape(-1, 16).T, (8, 1)).astype(np.uint16)


def unstriped(offs):
    return offs[:16].T.reshape(-1).astype(np.int64)


E2M1 = np.array([0.0, 0.5, 1.0, 1.5, 2.0, 3.0, 4.0, 6.0, -0.0, -0.5, -1.0, -1.5, -2.0, -3.0, -4.0, -6.0])


def pack_weight(w, fmt):
    k, n = w.shape
    w = f64(np.asarray(w, np.float32).astype(ml_dtypes.bfloat16)).reshape(k // 32, 32, n)
    amax = np.abs(w).max(1)
    if fmt == "e4m3":
        byte = np.frexp(amax)[1] - 1 + 127 - 7
    else:
        mant, ex = np.frexp(amax / 6.0)
        byte = np.where(mant > 0.5, ex, ex - 1) + 127
    byte = np.clip(np.where(amax > 0, byte, 1), 1, 254)
    scaled = (w * np.exp2(127.0 - byte)[:, None, :]).reshape(k, n).astype(np.float32)
    by_word = np.ascontiguousarray(scaled.reshape(k // 512, 128, 4, n).transpose(0, 1, 3, 2))
    if fmt == "e4m3":
        words = by_word.astype(ml_dtypes.float8_e4m3fn).view(np.uint8)
    else:
        c = by_word.astype(ml_dtypes.float4_e2m1fn).view(np.uint8) & 0xF
        words = (c[..., 0::2] | (c[..., 1::2] << 4)).reshape(k // 512, 128, 2 * n)
    return np.ascontiguousarray(words), np.ascontiguousarray(byte.astype(np.uint8).reshape(k // 512, 16, n))


def unpack_weight(words, scales, fmt):
    g, _, n = scales.shape
    words = np.ascontiguousarray(words).reshape(g, 128, n, -1)
    if fmt == "e4m3":
        vals = words.view(ml_dtypes.float8_e4m3fn).astype(np.float64)
    else:
        nib = np.empty((g, 128, n, 4), np.uint8)
        nib[..., 0::2] = words & 0xF
        nib[..., 1::2] = words >> 4
        vals = E2M1[nib]
    vals = vals * np.repeat(np.exp2(scales.astype(np.float64) - 127.0), 8, axis=1)[..., None]
    return vals.transpose(0, 1, 3, 2).reshape(g * 512, n)


def bf(x):
    return np.asarray(x, np.float32).astype(ml_dtypes.bfloat16)


def planes(Y):
    r, m = Y.shape
    b = f64(bf(Y)).reshape(r // 32, 32, m)
    amax = np.abs(b).max(1)
    byte = np.clip(np.where(amax > 0, np.frexp(amax)[1] - 1 + 127 - 7, 1), 1, 254)
    codes = (b * np.exp2(127.0 - byte)[:, None, :]).reshape(r, m).astype(np.float32).astype(ml_dtypes.float8_e4m3fn).view(np.uint8)
    words = codes.reshape(r // 512, 128, 4, m).transpose(0, 1, 3, 2)
    return np.ascontiguousarray(words), np.ascontiguousarray(byte.astype(np.uint8).reshape(r // 512, 16, m))


K, T, J, L, N = 1024, 2048, 512, 512, 512


def setup_inputs():
    n = np.random.standard_normal
    idx = np.random.permutation(T)[:J]
    fk = mx_kscale(K)
    fl = mx_kscale(L)
    wap = pack_weight(n((K, N)) * 1 / np.sqrt(K) * fk[:, None], "e4m3")
    cxp = pack_weight(n((L, J)) / fl[:, None], "e2m1")
    wcp = pack_weight(n((L, N)) * 1 / np.sqrt(L) * fl[:, None], "e4m3")
    return {
        "xf": (n((K, T))).astype(np.float32),
        "ga": (np.random.uniform(0.4, 1.2, (1, J))).astype(np.float32),
        "fk": (np.random.uniform(0.5, 2.0, (K, 1)) / fk[:, None]).astype(np.float32),
        "wa_words": wap[0],
        "wa_scales": wap[1],
        "cx_words": cxp[0],
        "cx_scales": cxp[1],
        "wc_words": wcp[0],
        "wc_scales": wcp[1],
        "offs": striped(idx),
    }


def reference(xf, ga, fk, wa_words, wa_scales, cx_words, cx_scales, wc_words, wc_scales, offs):
    idx = unstriped(offs)
    wau = unpack_weight(wa_words, wa_scales, "e4m3")
    cxu = unpack_weight(cx_words, cx_scales, "e2m1")
    wcu = unpack_weight(wc_words, wc_scales, "e4m3")
    xs = f64(xf)[:, idx] * f64(ga) * f64(fk)
    xsq = mxq(xs, 0, "e4m3")
    p = wau.T @ xsq
    q = wcu.T @ cxu
    y = np.maximum(p, 0.0) + q
    words, scales = planes(y)
    return y, words, scales

@@ -1,0 +1,228 @@
+from contextlib import ExitStack
+
+import concourse.mybir as mybir
+from concourse.masks import make_identity
+
+K, T, J, L, N = 1024, 2048, 512, 512, 512
+FLOPS = 2 * (K + L) * N * J
+
+F32 = mybir.dt.float32
+BF16 = mybir.dt.bfloat16
+I32 = mybir.dt.int32
+U32 = mybir.dt.uint32
+U16 = mybir.dt.uint16
+U8 = mybir.dt.uint8
+FP8X4 = mybir.dt.float8_e4m3fn_x4
+FP4X4 = mybir.dt.float4_e2m1fn_x4
+ALU = mybir.AluOpType
+COPY = mybir.ActivationFunctionType.Copy
+
+P = 128
+PACK = 4
+PASSES = K // (P * PACK)
+QUADS = 4
+SLICE = 128
+SLICES = J // SLICE
+OFF_COLS = SLICE // 16
+
+
+def interleave(nc, dst, src):
+    nc.scalar.copy(
+        dst.rearrange("p (c i) t -> p c t i", i=4),
+        src.rearrange("p t (c i) -> p c t i", i=4),
+    )
+
+
+def deal_words(nc, dst, src):
+    nc.vector.tensor_copy(
+        dst.bitcast(I32).rearrange("p (t c i) -> p c t i", t=PACK, i=4),
+        src.rearrange("p (c i t) -> p c t i", t=PACK, i=4),
+    )
+
+
+def tile_list_expert_gated_inputs_pl_kernel(
+    tc, xf, ga, fk, wa_words, wa_scales, cx_words, cx_scales, wc_words, wc_scales, offs, out_0, out_1, out_2
+):
+    nc = tc.nc
+    with ExitStack() as ctx:
+        keep = ctx.enter_context(tc.tile_pool(name="keep", bufs=1))
+        psum = ctx.enter_context(tc.psum_pool(name="psum", bufs=1))
+        psum_q = ctx.enter_context(tc.psum_pool(name="psum_q", bufs=2))
+
+        xf_rows = xf.rearrange("(a p t) c -> a t p c", a=PASSES, t=PACK)
+        planes = [
+            [keep.tile([P, T], F32, name=f"plane_{a}_{t}") for t in range(PACK)] for a in range(PASSES)
+        ]
+        offsets = keep.tile([P, J // 16], U16, name="offsets")
+        ga_cols = keep.tile([P, PACK], F32, name="ga_cols")
+        fk_cols = keep.tile([P, PASSES, PACK], F32, name="fk_cols")
+        wc_raw = keep.tile([P, N], I32, name="wc_raw")
+        wa_raw = keep.tile([P, PASSES, N], I32, name="wa_raw")
+        cx_codes = keep.tile([P, 2 * J], U8, name="cx_codes", align_bytes=64)
+        w_scale_raw = keep.tile([P, N], U8, name="w_scale_raw")
+        cx_scale = keep.tile([P, J], U8, name="cx_scale", align_bytes=64)
+        ident = keep.tile([P, P], F32, name="ident")
+
+        make_identity(nc, ident[:])
+        nc.vector.memset(w_scale_raw[:].bitcast(I32), 0)
+        nc.vector.memset(cx_scale[:].bitcast(I32), 0)
+
+        nc.sync.dma_start(wc_raw[:], wc_words[0].rearrange("p n t -> p (n t)").bitcast(I32))
+        nc.sync.dma_start(ga_cols[:], ga.rearrange("o (p c) -> (o p) c", c=PACK))
+        nc.sync.dma_start(fk_cols[:], fk.rearrange("(a p t) o -> p a (t o)", a=PASSES, t=PACK))
+        nc.sync.dma_start(offsets[:], offs)
+        nc.sync.dma_start(wa_raw[:], wa_words.rearrange("a p n t -> p a (n t)").bitcast(I32))
+        nc.sync.dma_start(planes[0][0][:], xf_rows[0, 0])
+        nc.sync.dma_start(planes[0][1][:], xf_rows[0, 1])
+        nc.sync.dma_start(cx_codes[:].bitcast(I32), cx_words[0].bitcast(I32))
+        nc.sync.dma_start(planes[0][2][:], xf_rows[0, 2])
+        nc.sync.dma_start(planes[0][3][:], xf_rows[0, 3])
+        for q in range(QUADS):
+            nc.sync.dma_start(
+                w_scale_raw[32 * q + 4 : 32 * q + 12, :].bitcast(I32),
+                wa_scales[:, 4 * q : 4 * q + 4, :].bitcast(I32),
+            )
+        for t in range(PACK):
+            nc.sync.dma_start(planes[1][t][:], xf_rows[1, t])
+        for tile, scales in ((w_scale_raw, wc_scales), (cx_scale, cx_scales)):
+            for q in range(QUADS):
+                nc.gpsimd.dma_start(
+                    tile[32 * q : 32 * q + 4, :].bitcast(I32), scales[0, 4 * q : 4 * q + 4, :].bitcast(I32)
+                )
+
+        ga_psum = psum.tile([P, PACK, P], F32, name="ga_psum")
+        for c in range(PACK):
+            nc.tensor.transpose(ga_psum[:, c, :], ga_cols[:, c : c + 1].to_broadcast([P, P]), ident[:])
+        factor = [
+            [keep.tile([P, J], F32, name=f"factor_{a}_{t}") for t in range(PACK)] for a in range(PASSES)
+        ]
+        for a in range(PASSES):
+            for t in range(PACK):
+                nc.scalar.activation(
+                    factor[a][t][:].rearrange("p (n c) -> p n c", c=PACK),
+                    ga_psum[:].rearrange("p c n -> p n c"),
+                    COPY,
+                    scale=fk_cols[:, a, t : t + 1],
+                )
+
+        xs0 = keep.tile([P, PACK, J], F32, name="xs0")
+        xs0_bf = keep.tile([P, J, PACK], BF16, name="xs0_bf", align_bytes=64)
+        xs0_codes = keep.tile([P, J], U32, name="xs0_codes", align_bytes=64)
+        xs0_scale = keep.tile([P, J], U8, name="xs0_scale", align_bytes=64)
+        for t in range(PACK - 1):
+            nc.vector.tensor_tensor(xs0[:, t, :], planes[0][t][:].indirect(offsets[:]), factor[0][t][:], ALU.mult)
+
+        w_scale = keep.tile([P, N], U8, name="w_scale", align_bytes=64)
+        wc_codes = keep.tile([P, N], U32, name="wc_codes", align_bytes=64)
+        nc.vector.tensor_copy(
+            w_scale[:].rearrange("p (t m) -> p t m", t=PACK), w_scale_raw[:].rearrange("p (m t) -> p t m", t=PACK)
+        )
+        deal_words(nc, wc_codes[:], wc_raw[:])
+        q_sb = keep.tile([P, SLICES, PACK, SLICE], F32, name="q_sb")
+        for t in range(PACK):
+            cols = slice(t * P, (t + 1) * P)
+            q_psum = psum_q.tile([P, J], F32, name="q_psum")
+            nc.tensor.matmul_mx(
+                out=q_psum[:],
+                lhsT=wc_codes[:, cols].bitcast(FP8X4),
+                lhsT_scale=w_scale[:, cols],
+                rhs=cx_codes[:].bitcast(FP4X4),
+                rhs_scale=cx_scale[:],
+                start=True,
+                stop=True,
+            )
+            nc.scalar.copy(q_sb[:, :, t, :], q_psum[:].rearrange("p (s j) -> p s j", s=SLICES))
+
+        t = PACK - 1
+        nc.vector.tensor_tensor(xs0[:, t, :], planes[0][t][:].indirect(offsets[:]), factor[0][t][:], ALU.mult)
+        interleave(nc, xs0_bf[:], xs0[:])
+        nc.vector.quantize_mx(
+            out=xs0_codes[:].bitcast(FP8X4), scales=xs0_scale[:], in_=xs0_bf[:].rearrange("p j t -> p (j t)")
+        )
+
+        xs1 = [keep.tile([P, PACK, SLICE], F32, name=f"xs1_{s}") for s in range(SLICES)]
+
+        def gather1(t, s):
+            nc.vector.tensor_tensor(
+                xs1[s][:, t, :],
+                planes[1][t][:].indirect(offsets[:, s * OFF_COLS : (s + 1) * OFF_COLS]),
+                factor[1][t][:, s * SLICE : (s + 1) * SLICE],
+                ALU.mult,
+            )
+
+        for t in range(PACK - 1):
+            for s in range(SLICES):
+                gather1(t, s)
+
+        wa_codes = [keep.tile([P, N], U32, name=f"wa_codes_{a}", align_bytes=64) for a in range(PASSES)]
+        for a in range(PASSES):
+            deal_words(nc, wa_codes[a][:], wa_raw[:, a, :])
+
+        p_psum = [psum.tile([P, PACK, SLICE], F32, name=f"p_psum_{s}") for s in range(SLICES)]
+
+        def product(a, s, codes, scale):
+            for t in range(PACK):
+                cols = slice(t * P, (t + 1) * P)
+                nc.tensor.matmul_mx(
+                    out=p_psum[s][:, t, :],
+                    lhsT=wa_codes[a][:, cols].bitcast(FP8X4),
+                    lhsT_scale=w_scale[4 * (a + 1) : P, cols],
+                    rhs=codes.bitcast(FP8X4),
+                    rhs_scale=scale,
+                    start=(a == 0 and t == 0),
+                    stop=(a == PASSES - 1 and t == PACK - 1),
+                )
+
+        for s in range(SLICES):
+            js = slice(s * SLICE, (s + 1) * SLICE)
+            product(0, s, xs0_codes[:, js], xs0_scale[:, js])
+
+        y_rows = out_0.rearrange("(p t) j -> p t j", t=PACK)
+        y_words = out_1[0].rearrange("p c r -> p (c r)").bitcast(I32)
+        y_scale = keep.tile([P, J], U8, name="y_scale", align_bytes=64)
+        y = [keep.tile([P, PACK, SLICE], F32, name=f"y_{s}") for s in range(SLICES)]
+
+        def front(s):
+            xs1_bf = keep.tile([P, SLICE, PACK], BF16, name=f"xs1_bf_{s}", align_bytes=64)
+            xs1_codes = keep.tile([P, SLICE], U32, name=f"xs1_codes_{s}", align_bytes=64)
+            xs1_scale = keep.tile([P, SLICE], U8, name=f"xs1_scale_{s}", align_bytes=64)
+            interleave(nc, xs1_bf[:], xs1[s][:])
+            nc.vector.quantize_mx(
+                out=xs1_codes[:].bitcast(FP8X4), scales=xs1_scale[:], in_=xs1_bf[:].rearrange("p j t -> p (j t)")
+            )
+            product(1, s, xs1_codes[:], xs1_scale[:])
+
+        def result(s):
+            js = slice(s * SLICE, (s + 1) * SLICE)
+            nc.vector.scalar_tensor_tensor(
+                y[s][:].rearrange("p t j -> p (t j)"),
+                p_psum[s][:].rearrange("p t j -> p (t j)"),
+                0.0,
+                q_sb[:, s, :, :].rearrange("p t j -> p (t j)"),
+                ALU.max,
+                ALU.add,
+            )
+            nc.sync.dma_start(y_rows[:, :, js], y[s][:])
+
+        def planes_out(s):
+            js = slice(s * SLICE, (s + 1) * SLICE)
+            y_bf = keep.tile([P, SLICE, PACK], BF16, name=f"y_bf_{s}", align_bytes=64)
+            y_codes = keep.tile([P, SLICE], U32, name=f"y_codes_{s}", align_bytes=64)
+            interleave(nc, y_bf[:], y[s][:])
+            nc.vector.quantize_mx(
+                out=y_codes[:].bitcast(FP8X4), scales=y_scale[:, js], in_=y_bf[:].rearrange("p j t -> p (j t)")
+            )
+            nc.sync.dma_start(y_words[:, js], y_codes[:].bitcast(I32))
+
+        for s in range(SLICES):
+            gather1(PACK - 1, s)
+        for step in range(SLICES + 3):
+            if step < SLICES:
+                front(step)
+            if 0 <= step - 2 < SLICES:
+                result(step - 2)
+            if 0 <= step - 3 < SLICES:
+                planes_out(step - 3)
+        for q in range(QUADS):
+            queue = nc.scalar if q % 2 == 0 else nc.sync
+            queue.dma_start(out_2[0, 4 * q : 4 * q + 4, :].bitcast(I32), y_scale[32 * q : 32 * q + 4, :].bitcast(I32))

@@ -67,28 +67,31 @@ def tile_list_expert_gated_inputs_pl_kernel(
         nc.vector.memset(w_scale_raw[:].bitcast(I32), 0)
         nc.vector.memset(cx_scale[:].bitcast(I32), 0)
 
-        nc.sync.dma_start(wc_raw[:], wc_words[0].rearrange("p n t -> p (n t)").bitcast(I32))
+        def load_scale_rows(queue, tile, first, scales, q):
+            rows = scales.shape[0] * 4
+            queue.dma_start(
+                tile[32 * q + first : 32 * q + first + rows, :].bitcast(I32),
+                scales[:, 4 * q : 4 * q + 4, :].bitcast(I32),
+            )
+
+        nc.sync.dma_start(wa_raw[:], wa_words.rearrange("a p n t -> p a (n t)").bitcast(I32))
         nc.sync.dma_start(ga_cols[:], ga.rearrange("o (p c) -> (o p) c", c=PACK))
         nc.sync.dma_start(fk_cols[:], fk.rearrange("(a p t) o -> p a (t o)", a=PASSES, t=PACK))
         nc.sync.dma_start(offsets[:], offs)
-        nc.sync.dma_start(wa_raw[:], wa_words.rearrange("a p n t -> p a (n t)").bitcast(I32))
         nc.sync.dma_start(planes[0][0][:], xf_rows[0, 0])
         nc.sync.dma_start(planes[0][1][:], xf_rows[0, 1])
+        nc.sync.dma_start(wc_raw[:], wc_words[0].rearrange("p n t -> p (n t)").bitcast(I32))
         nc.sync.dma_start(cx_codes[:].bitcast(I32), cx_words[0].bitcast(I32))
+        for q in range(QUADS):
+            load_scale_rows(nc.sync, w_scale_raw, 0, wc_scales, q)
         nc.sync.dma_start(planes[0][2][:], xf_rows[0, 2])
         nc.sync.dma_start(planes[0][3][:], xf_rows[0, 3])
         for q in range(QUADS):
-            nc.sync.dma_start(
-                w_scale_raw[32 * q + 4 : 32 * q + 12, :].bitcast(I32),
-                wa_scales[:, 4 * q : 4 * q + 4, :].bitcast(I32),
-            )
+            load_scale_rows(nc.sync, w_scale_raw, 4, wa_scales, q)
+        for q in range(QUADS):
+            load_scale_rows(nc.sync if q < 2 else nc.gpsimd, cx_scale, 0, cx_scales, q)
         for t in range(PACK):
             nc.sync.dma_start(planes[1][t][:], xf_rows[1, t])
-        for tile, scales in ((w_scale_raw, wc_scales), (cx_scale, cx_scales)):
-            for q in range(QUADS):
-                nc.gpsimd.dma_start(
-                    tile[32 * q : 32 * q + 4, :].bitcast(I32), scales[0, 4 * q : 4 * q + 4, :].bitcast(I32)
-                )
 
         ga_psum = psum.tile([P, PACK, P], F32, name="ga_psum")
         for c in range(PACK):
@@ -140,19 +143,23 @@ def tile_list_expert_gated_inputs_pl_kernel(
             out=xs0_codes[:].bitcast(FP8X4), scales=xs0_scale[:], in_=xs0_bf[:].rearrange("p j t -> p (j t)")
         )
 
-        xs1 = [keep.tile([P, PACK, SLICE], F32, name=f"xs1_{s}") for s in range(SLICES)]
+        xs1_lo = keep.tile([P, 2, J], F32, name="xs1_lo")
+        xs1_hi = [keep.tile([P, 2, SLICE], F32, name=f"xs1_hi_{s}") for s in range(SLICES)]
+        xs1_bf = keep.tile([P, J, PACK], BF16, name="xs1_bf", align_bytes=64)
 
-        def gather1(t, s):
+        def gather_hi(t, s):
             nc.vector.tensor_tensor(
-                xs1[s][:, t, :],
+                xs1_hi[s][:, t - 2, :],
                 planes[1][t][:].indirect(offsets[:, s * OFF_COLS : (s + 1) * OFF_COLS]),
                 factor[1][t][:, s * SLICE : (s + 1) * SLICE],
                 ALU.mult,
             )
 
-        for t in range(PACK - 1):
-            for s in range(SLICES):
-                gather1(t, s)
+        for t in range(2):
+            nc.vector.tensor_tensor(xs1_lo[:, t, :], planes[1][t][:].indirect(offsets[:]), factor[1][t][:], ALU.mult)
+        nc.scalar.copy(xs1_bf[:, :, 0:2], xs1_lo[:].rearrange("p t j -> p j t"))
+        for s in range(SLICES):
+            gather_hi(2, s)
 
         wa_codes = [keep.tile([P, N], U32, name=f"wa_codes_{a}", align_bytes=64) for a in range(PASSES)]
         for a in range(PASSES):
@@ -180,15 +187,16 @@ def tile_list_expert_gated_inputs_pl_kernel(
         y_rows = out_0.rearrange("(p t) j -> p t j", t=PACK)
         y_words = out_1[0].rearrange("p c r -> p (c r)").bitcast(I32)
         y_scale = keep.tile([P, J], U8, name="y_scale", align_bytes=64)
+        y_codes = keep.tile([P, J], U32, name="y_codes", align_bytes=64)
         y = [keep.tile([P, PACK, SLICE], F32, name=f"y_{s}") for s in range(SLICES)]
 
         def front(s):
-            xs1_bf = keep.tile([P, SLICE, PACK], BF16, name=f"xs1_bf_{s}", align_bytes=64)
+            js = slice(s * SLICE, (s + 1) * SLICE)
             xs1_codes = keep.tile([P, SLICE], U32, name=f"xs1_codes_{s}", align_bytes=64)
             xs1_scale = keep.tile([P, SLICE], U8, name=f"xs1_scale_{s}", align_bytes=64)
-            interleave(nc, xs1_bf[:], xs1[s][:])
+            nc.scalar.copy(xs1_bf[:, js, 2:4], xs1_hi[s][:].rearrange("p t j -> p j t"))
             nc.vector.quantize_mx(
-                out=xs1_codes[:].bitcast(FP8X4), scales=xs1_scale[:], in_=xs1_bf[:].rearrange("p j t -> p (j t)")
+                out=xs1_codes[:].bitcast(FP8X4), scales=xs1_scale[:], in_=xs1_bf[:, js, :].rearrange("p j t -> p (j t)")
             )
             product(1, s, xs1_codes[:], xs1_scale[:])
 
@@ -207,15 +215,16 @@ def tile_list_expert_gated_inputs_pl_kernel(
         def planes_out(s):
             js = slice(s * SLICE, (s + 1) * SLICE)
             y_bf = keep.tile([P, SLICE, PACK], BF16, name=f"y_bf_{s}", align_bytes=64)
-            y_codes = keep.tile([P, SLICE], U32, name=f"y_codes_{s}", align_bytes=64)
             interleave(nc, y_bf[:], y[s][:])
             nc.vector.quantize_mx(
-                out=y_codes[:].bitcast(FP8X4), scales=y_scale[:, js], in_=y_bf[:].rearrange("p j t -> p (j t)")
+                out=y_codes[:, js].bitcast(FP8X4), scales=y_scale[:, js], in_=y_bf[:].rearrange("p j t -> p (j t)")
             )
-            nc.sync.dma_start(y_words[:, js], y_codes[:].bitcast(I32))
+            if s >= SLICES - 2:
+                done = slice(0, J - SLICE) if s == SLICES - 2 else js
+                nc.sync.dma_start(y_words[:, done], y_codes[:, done].bitcast(I32))
 
         for s in range(SLICES):
-            gather1(PACK - 1, s)
+            gather_hi(3, s)
         for step in range(SLICES + 3):
             if step < SLICES:
                 front(step)

@@ -26,8 +26,8 @@ SLICES = J // SLICE
 OFF_COLS = SLICE // 16
 
 
-def interleave(nc, dst, src):
-    nc.scalar.copy(
+def interleave(copy, dst, src):
+    copy(
         dst.rearrange("p (c i) t -> p c t i", i=4),
         src.rearrange("p t (c i) -> p c t i", i=4),
     )
@@ -55,7 +55,7 @@ def tile_list_expert_gated_inputs_pl_kernel(
         ]
         offsets = keep.tile([P, J // 16], U16, name="offsets")
         ga_cols = keep.tile([P, PACK], F32, name="ga_cols")
-        fk_cols = keep.tile([P, PASSES, PACK], F32, name="fk_cols")
+        fk_cols = keep.tile([P, PASSES, 2 * PACK], F32, name="fk_cols")
         wc_raw = keep.tile([P, N], I32, name="wc_raw")
         wa_raw = keep.tile([P, PASSES, N], I32, name="wa_raw")
         cx_codes = keep.tile([P, 2 * J], U8, name="cx_codes", align_bytes=64)
@@ -74,30 +74,32 @@ def tile_list_expert_gated_inputs_pl_kernel(
                 scales[:, 4 * q : 4 * q + 4, :].bitcast(I32),
             )
 
-        nc.sync.dma_start(wa_raw[:], wa_words.rearrange("a p n t -> p a (n t)").bitcast(I32))
+        nc.sync.dma_start(wc_raw[:], wc_words[0].rearrange("p n t -> p (n t)").bitcast(I32))
         nc.sync.dma_start(ga_cols[:], ga.rearrange("o (p c) -> (o p) c", c=PACK))
-        nc.sync.dma_start(fk_cols[:], fk.rearrange("(a p t) o -> p a (t o)", a=PASSES, t=PACK))
+        nc.sync.dma_start(fk_cols[:, :, 0:PACK], fk.rearrange("(a p t) o -> p a (t o)", a=PASSES, t=PACK))
         nc.sync.dma_start(offsets[:], offs)
         nc.sync.dma_start(planes[0][0][:], xf_rows[0, 0])
         nc.sync.dma_start(planes[0][1][:], xf_rows[0, 1])
-        nc.sync.dma_start(wc_raw[:], wc_words[0].rearrange("p n t -> p (n t)").bitcast(I32))
-        nc.sync.dma_start(cx_codes[:].bitcast(I32), cx_words[0].bitcast(I32))
-        for q in range(QUADS):
+        for q in range(2):
             load_scale_rows(nc.sync, w_scale_raw, 0, wc_scales, q)
         nc.sync.dma_start(planes[0][2][:], xf_rows[0, 2])
+        for q in range(2, QUADS):
+            load_scale_rows(nc.sync, w_scale_raw, 0, wc_scales, q)
+        nc.sync.dma_start(cx_codes[:].bitcast(I32), cx_words[0].bitcast(I32))
         nc.sync.dma_start(planes[0][3][:], xf_rows[0, 3])
+        nc.sync.dma_start(wa_raw[:], wa_words.rearrange("a p n t -> p a (n t)").bitcast(I32))
         for q in range(QUADS):
             load_scale_rows(nc.sync, w_scale_raw, 4, wa_scales, q)
-        for q in range(QUADS):
-            load_scale_rows(nc.sync if q < 2 else nc.gpsimd, cx_scale, 0, cx_scales, q)
         for t in range(PACK):
             nc.sync.dma_start(planes[1][t][:], xf_rows[1, t])
+        for q in range(QUADS):
+            load_scale_rows(nc.gpsimd, cx_scale, 0, cx_scales, q)
 
         ga_psum = psum.tile([P, PACK, P], F32, name="ga_psum")
         for c in range(PACK):
             nc.tensor.transpose(ga_psum[:, c, :], ga_cols[:, c : c + 1].to_broadcast([P, P]), ident[:])
         factor = [
-            [keep.tile([P, J], F32, name=f"factor_{a}_{t}") for t in range(PACK)] for a in range(PASSES)
+            [keep.tile([P, J], F32, name=f"factor_{a}_{t}", tag=f"factor_{a}_{t}", align_bytes=64) for t in range(PACK)] for a in range(PASSES)
         ]
         for a in range(PASSES):
             for t in range(PACK):
@@ -138,7 +140,7 @@ def tile_list_expert_gated_inputs_pl_kernel(
 
         t = PACK - 1
         nc.vector.tensor_tensor(xs0[:, t, :], planes[0][t][:].indirect(offsets[:]), factor[0][t][:], ALU.mult)
-        interleave(nc, xs0_bf[:], xs0[:])
+        interleave(nc.scalar.copy, xs0_bf[:], xs0[:])
         nc.vector.quantize_mx(
             out=xs0_codes[:].bitcast(FP8X4), scales=xs0_scale[:], in_=xs0_bf[:].rearrange("p j t -> p (j t)")
         )
@@ -161,7 +163,10 @@ def tile_list_expert_gated_inputs_pl_kernel(
         for s in range(SLICES):
             gather_hi(2, s)
 
-        wa_codes = [keep.tile([P, N], U32, name=f"wa_codes_{a}", align_bytes=64) for a in range(PASSES)]
+        wa_codes = [
+            keep.tile([P, N], U32, name="wa_codes_0", tag="factor_1_1", align_bytes=64),
+            keep.tile([P, N], U32, name="wa_codes_1", align_bytes=64),
+        ]
         for a in range(PASSES):
             deal_words(nc, wa_codes[a][:], wa_raw[:, a, :])
 
@@ -215,23 +220,22 @@ def tile_list_expert_gated_inputs_pl_kernel(
         def planes_out(s):
             js = slice(s * SLICE, (s + 1) * SLICE)
             y_bf = keep.tile([P, SLICE, PACK], BF16, name=f"y_bf_{s}", align_bytes=64)
-            interleave(nc, y_bf[:], y[s][:])
+            interleave(nc.vector.tensor_copy if s == SLICES - 1 else nc.scalar.copy, y_bf[:], y[s][:])
             nc.vector.quantize_mx(
                 out=y_codes[:, js].bitcast(FP8X4), scales=y_scale[:, js], in_=y_bf[:].rearrange("p j t -> p (j t)")
             )
-            if s >= SLICES - 2:
-                done = slice(0, J - SLICE) if s == SLICES - 2 else js
+            if s % 2 == 1:
+                done = slice((s - 1) * SLICE, (s + 1) * SLICE)
                 nc.sync.dma_start(y_words[:, done], y_codes[:, done].bitcast(I32))
 
         for s in range(SLICES):
             gather_hi(3, s)
-        for step in range(SLICES + 3):
-            if step < SLICES:
-                front(step)
-            if 0 <= step - 2 < SLICES:
-                result(step - 2)
-            if 0 <= step - 3 < SLICES:
-                planes_out(step - 3)
+        for s in range(SLICES):
+            front(s)
+        for s in range(SLICES):
+            result(s)
+        for s in range(SLICES):
+            planes_out(s)
         for q in range(QUADS):
             queue = nc.scalar if q % 2 == 0 else nc.sync
             queue.dma_start(out_2[0, 4 * q : 4 * q + 4, :].bitcast(I32), y_scale[32 * q : 32 * q + 4, :].bitcast(I32))

@@ -24,6 +24,7 @@ QUADS = 4
 SLICE = 128
 SLICES = J // SLICE
 OFF_COLS = SLICE // 16
+HALF = J // 2
 
 
 def interleave(copy, dst, src):
@@ -123,7 +124,7 @@ def tile_list_expert_gated_inputs_pl_kernel(
             w_scale[:].rearrange("p (t m) -> p t m", t=PACK), w_scale_raw[:].rearrange("p (m t) -> p t m", t=PACK)
         )
         deal_words(nc, wc_codes[:], wc_raw[:])
-        q_sb = keep.tile([P, SLICES, PACK, SLICE], F32, name="q_sb")
+        q_sb = keep.tile([P, 2, PACK, HALF], F32, name="q_sb")
         for t in range(PACK):
             cols = slice(t * P, (t + 1) * P)
             q_psum = psum_q.tile([P, J], F32, name="q_psum")
@@ -136,7 +137,7 @@ def tile_list_expert_gated_inputs_pl_kernel(
                 start=True,
                 stop=True,
             )
-            nc.scalar.copy(q_sb[:, :, t, :], q_psum[:].rearrange("p (s j) -> p s j", s=SLICES))
+            nc.scalar.copy(q_sb[:, :, t, :], q_psum[:].rearrange("p (h j) -> p h j", h=2))
 
         t = PACK - 1
         nc.vector.tensor_tensor(xs0[:, t, :], planes[0][t][:].indirect(offsets[:]), factor[0][t][:], ALU.mult)
@@ -170,30 +171,31 @@ def tile_list_expert_gated_inputs_pl_kernel(
         for a in range(PASSES):
             deal_words(nc, wa_codes[a][:], wa_raw[:, a, :])
 
-        p_psum = [psum.tile([P, PACK, SLICE], F32, name=f"p_psum_{s}") for s in range(SLICES)]
+        p_psum = [[psum.tile([P, 2, HALF], F32, name=f"p_psum_{h}_{u}") for u in range(2)] for h in range(2)]
 
-        def product(a, s, codes, scale):
+        def product(a, j0, width, codes, scale):
+            h, c0 = divmod(j0, HALF)
             for t in range(PACK):
                 cols = slice(t * P, (t + 1) * P)
                 nc.tensor.matmul_mx(
-                    out=p_psum[s][:, t, :],
+                    out=p_psum[h][t // 2][:, t % 2, c0 : c0 + width],
                     lhsT=wa_codes[a][:, cols].bitcast(FP8X4),
                     lhsT_scale=w_scale[4 * (a + 1) : P, cols],
                     rhs=codes.bitcast(FP8X4),
                     rhs_scale=scale,
-                    start=(a == 0 and t == 0),
-                    stop=(a == PASSES - 1 and t == PACK - 1),
+                    start=(a == 0 and t % 2 == 0),
+                    stop=(a == PASSES - 1 and c0 + width == HALF and t % 2 == 1),
                 )
 
-        for s in range(SLICES):
-            js = slice(s * SLICE, (s + 1) * SLICE)
-            product(0, s, xs0_codes[:, js], xs0_scale[:, js])
+        for h in range(2):
+            js = slice(h * HALF, (h + 1) * HALF)
+            product(0, h * HALF, HALF, xs0_codes[:, js], xs0_scale[:, js])
 
         y_rows = out_0.rearrange("(p t) j -> p t j", t=PACK)
         y_words = out_1[0].rearrange("p c r -> p (c r)").bitcast(I32)
         y_scale = keep.tile([P, J], U8, name="y_scale", align_bytes=64)
         y_codes = keep.tile([P, J], U32, name="y_codes", align_bytes=64)
-        y = [keep.tile([P, PACK, SLICE], F32, name=f"y_{s}") for s in range(SLICES)]
+        y = [keep.tile([P, PACK, HALF], F32, name=f"y_{h}") for h in range(2)]
 
         def front(s):
             js = slice(s * SLICE, (s + 1) * SLICE)
@@ -203,39 +205,41 @@ def tile_list_expert_gated_inputs_pl_kernel(
             nc.vector.quantize_mx(
                 out=xs1_codes[:].bitcast(FP8X4), scales=xs1_scale[:], in_=xs1_bf[:, js, :].rearrange("p j t -> p (j t)")
             )
-            product(1, s, xs1_codes[:], xs1_scale[:])
+            product(1, s * SLICE, SLICE, xs1_codes[:], xs1_scale[:])
 
-        def result(s):
-            js = slice(s * SLICE, (s + 1) * SLICE)
+        def result(h, u):
+            ts = slice(2 * u, 2 * u + 2)
             nc.vector.scalar_tensor_tensor(
-                y[s][:].rearrange("p t j -> p (t j)"),
-                p_psum[s][:].rearrange("p t j -> p (t j)"),
+                y[h][:, ts, :].rearrange("p t j -> p (t j)"),
+                p_psum[h][u][:].rearrange("p t j -> p (t j)"),
                 0.0,
-                q_sb[:, s, :, :].rearrange("p t j -> p (t j)"),
+                q_sb[:, h, ts, :].rearrange("p t j -> p (t j)"),
                 ALU.max,
                 ALU.add,
             )
-            nc.sync.dma_start(y_rows[:, :, js], y[s][:])
+            nc.sync.dma_start(y_rows[:, ts, h * HALF : (h + 1) * HALF], y[h][:, ts, :])
 
-        def planes_out(s):
-            js = slice(s * SLICE, (s + 1) * SLICE)
-            y_bf = keep.tile([P, SLICE, PACK], BF16, name=f"y_bf_{s}", align_bytes=64)
-            interleave(nc.vector.tensor_copy if s == SLICES - 1 else nc.scalar.copy, y_bf[:], y[s][:])
+        def planes_out(copy, j0, width):
+            h, c0 = divmod(j0, HALF)
+            js = slice(j0, j0 + width)
+            y_bf = keep.tile([P, width, PACK], BF16, name=f"y_bf_{j0}", align_bytes=64)
+            interleave(copy, y_bf[:], y[h][:, :, c0 : c0 + width])
             nc.vector.quantize_mx(
                 out=y_codes[:, js].bitcast(FP8X4), scales=y_scale[:, js], in_=y_bf[:].rearrange("p j t -> p (j t)")
             )
-            if s % 2 == 1:
-                done = slice((s - 1) * SLICE, (s + 1) * SLICE)
-                nc.sync.dma_start(y_words[:, done], y_codes[:, done].bitcast(I32))
 
         for s in range(SLICES):
             gather_hi(3, s)
         for s in range(SLICES):
             front(s)
-        for s in range(SLICES):
-            result(s)
-        for s in range(SLICES):
-            planes_out(s)
+        for h in range(2):
+            for u in range(2):
+                result(h, u)
+        planes_out(nc.scalar.copy, 0, HALF)
+        nc.sync.dma_start(y_words[:, 0:HALF], y_codes[:, 0:HALF].bitcast(I32))
+        planes_out(nc.vector.tensor_copy, HALF + SLICE, SLICE)
+        planes_out(nc.scalar.copy, HALF, SLICE)
+        nc.sync.dma_start(y_words[:, HALF:J], y_codes[:, HALF:J].bitcast(I32))
         for q in range(QUADS):
             queue = nc.scalar if q % 2 == 0 else nc.sync
             queue.dma_start(out_2[0, 4 * q : 4 * q + 4, :].bitcast(I32), y_scale[32 * q : 32 * q + 4, :].bitcast(I32))

@@ -19,25 +19,36 @@ COPY = mybir.ActivationFunctionType.Copy
 
 P = 128
 PACK = 4
+PAIR = 2
 PASSES = K // (P * PACK)
 QUADS = 4
+SCALE_ROWS = 4
+LINE = 4
 SLICE = 128
 SLICES = J // SLICE
-OFF_COLS = SLICE // 16
+LIST_COLS = SLICE // 16
 HALF = J // 2
 
 
 def interleave(copy, dst, src):
     copy(
-        dst.rearrange("p (c i) t -> p c t i", i=4),
-        src.rearrange("p t (c i) -> p c t i", i=4),
+        dst.rearrange("p (c i) t -> p c t i", i=LINE),
+        src.rearrange("p t (c i) -> p c t i", i=LINE),
     )
 
 
 def deal_words(nc, dst, src):
     nc.vector.tensor_copy(
-        dst.bitcast(I32).rearrange("p (t c i) -> p c t i", t=PACK, i=4),
-        src.rearrange("p (c i t) -> p c t i", t=PACK, i=4),
+        dst.bitcast(I32).rearrange("p (t c i) -> p c t i", t=PACK, i=LINE),
+        src.rearrange("p (c i t) -> p c t i", t=PACK, i=LINE),
+    )
+
+
+def load_scale_rows(queue, tile, first_row, scales, quad):
+    rows = scales.shape[0] * SCALE_ROWS
+    queue.dma_start(
+        tile[32 * quad + first_row : 32 * quad + first_row + rows, :].bitcast(I32),
+        scales[:, SCALE_ROWS * quad : SCALE_ROWS * (quad + 1), :].bitcast(I32),
     )
 
 
@@ -51,14 +62,12 @@ def tile_list_expert_gated_inputs_pl_kernel(
         psum_q = ctx.enter_context(tc.psum_pool(name="psum_q", bufs=2))
 
         xf_rows = xf.rearrange("(a p t) c -> a t p c", a=PASSES, t=PACK)
-        planes = [
-            [keep.tile([P, T], F32, name=f"plane_{a}_{t}") for t in range(PACK)] for a in range(PASSES)
-        ]
+        xf_tiles = [[keep.tile([P, T], F32, name=f"xf_{a}_{t}") for t in range(PACK)] for a in range(PASSES)]
         offsets = keep.tile([P, J // 16], U16, name="offsets")
         ga_cols = keep.tile([P, PACK], F32, name="ga_cols")
         fk_cols = keep.tile([P, PASSES, 2 * PACK], F32, name="fk_cols")
         wc_raw = keep.tile([P, N], I32, name="wc_raw")
-        wa_raw = keep.tile([P, PASSES, N], I32, name="wa_raw")
+        wa_raw = [keep.tile([P, N], I32, name=f"wa_raw_{a}") for a in range(PASSES)]
         cx_codes = keep.tile([P, 2 * J], U8, name="cx_codes", align_bytes=64)
         w_scale_raw = keep.tile([P, N], U8, name="w_scale_raw")
         cx_scale = keep.tile([P, J], U8, name="cx_scale", align_bytes=64)
@@ -68,39 +77,34 @@ def tile_list_expert_gated_inputs_pl_kernel(
         nc.vector.memset(w_scale_raw[:].bitcast(I32), 0)
         nc.vector.memset(cx_scale[:].bitcast(I32), 0)
 
-        def load_scale_rows(queue, tile, first, scales, q):
-            rows = scales.shape[0] * 4
-            queue.dma_start(
-                tile[32 * q + first : 32 * q + first + rows, :].bitcast(I32),
-                scales[:, 4 * q : 4 * q + 4, :].bitcast(I32),
-            )
-
         nc.sync.dma_start(wc_raw[:], wc_words[0].rearrange("p n t -> p (n t)").bitcast(I32))
         nc.sync.dma_start(ga_cols[:], ga.rearrange("o (p c) -> (o p) c", c=PACK))
         nc.sync.dma_start(fk_cols[:, :, 0:PACK], fk.rearrange("(a p t) o -> p a (t o)", a=PASSES, t=PACK))
         nc.sync.dma_start(offsets[:], offs)
-        nc.sync.dma_start(planes[0][0][:], xf_rows[0, 0])
-        nc.sync.dma_start(planes[0][1][:], xf_rows[0, 1])
-        for q in range(2):
-            load_scale_rows(nc.sync, w_scale_raw, 0, wc_scales, q)
-        nc.sync.dma_start(planes[0][2][:], xf_rows[0, 2])
-        for q in range(2, QUADS):
-            load_scale_rows(nc.sync, w_scale_raw, 0, wc_scales, q)
+        nc.sync.dma_start(xf_tiles[0][0][:], xf_rows[0, 0])
+        nc.sync.dma_start(xf_tiles[0][1][:], xf_rows[0, 1])
+        for quad in range(QUADS // 2):
+            load_scale_rows(nc.sync, w_scale_raw, 0, wc_scales, quad)
+        nc.sync.dma_start(xf_tiles[0][2][:], xf_rows[0, 2])
+        for quad in range(QUADS // 2, QUADS):
+            load_scale_rows(nc.sync, w_scale_raw, 0, wc_scales, quad)
         nc.sync.dma_start(cx_codes[:].bitcast(I32), cx_words[0].bitcast(I32))
-        nc.sync.dma_start(planes[0][3][:], xf_rows[0, 3])
-        nc.sync.dma_start(wa_raw[:], wa_words.rearrange("a p n t -> p a (n t)").bitcast(I32))
-        for q in range(QUADS):
-            load_scale_rows(nc.sync, w_scale_raw, 4, wa_scales, q)
+        nc.sync.dma_start(xf_tiles[0][3][:], xf_rows[0, 3])
+        nc.sync.dma_start(wa_raw[0][:], wa_words[0].rearrange("p n t -> p (n t)").bitcast(I32))
+        for quad in range(QUADS):
+            load_scale_rows(nc.sync, w_scale_raw, SCALE_ROWS, wa_scales, quad)
         for t in range(PACK):
-            nc.sync.dma_start(planes[1][t][:], xf_rows[1, t])
-        for q in range(QUADS):
-            load_scale_rows(nc.gpsimd, cx_scale, 0, cx_scales, q)
+            nc.sync.dma_start(xf_tiles[1][t][:], xf_rows[1, t])
+        nc.sync.dma_start(wa_raw[1][:], wa_words[1].rearrange("p n t -> p (n t)").bitcast(I32))
+        for quad in range(QUADS):
+            load_scale_rows(nc.gpsimd, cx_scale, 0, cx_scales, quad)
 
         ga_psum = psum.tile([P, PACK, P], F32, name="ga_psum")
         for c in range(PACK):
             nc.tensor.transpose(ga_psum[:, c, :], ga_cols[:, c : c + 1].to_broadcast([P, P]), ident[:])
         factor = [
-            [keep.tile([P, J], F32, name=f"factor_{a}_{t}", tag=f"factor_{a}_{t}", align_bytes=64) for t in range(PACK)] for a in range(PASSES)
+            [keep.tile([P, J], F32, name=f"factor_{a}_{t}", tag=f"factor_{a}_{t}", align_bytes=64) for t in range(PACK)]
+            for a in range(PASSES)
         ]
         for a in range(PASSES):
             for t in range(PACK):
@@ -115,8 +119,12 @@ def tile_list_expert_gated_inputs_pl_kernel(
         xs0_bf = keep.tile([P, J, PACK], BF16, name="xs0_bf", align_bytes=64)
         xs0_codes = keep.tile([P, J], U32, name="xs0_codes", align_bytes=64)
         xs0_scale = keep.tile([P, J], U8, name="xs0_scale", align_bytes=64)
+
+        def gather_pass0(t):
+            nc.vector.tensor_tensor(xs0[:, t, :], xf_tiles[0][t][:].indirect(offsets[:]), factor[0][t][:], ALU.mult)
+
         for t in range(PACK - 1):
-            nc.vector.tensor_tensor(xs0[:, t, :], planes[0][t][:].indirect(offsets[:]), factor[0][t][:], ALU.mult)
+            gather_pass0(t)
 
         w_scale = keep.tile([P, N], U8, name="w_scale", align_bytes=64)
         wc_codes = keep.tile([P, N], U32, name="wc_codes", align_bytes=64)
@@ -124,7 +132,7 @@ def tile_list_expert_gated_inputs_pl_kernel(
             w_scale[:].rearrange("p (t m) -> p t m", t=PACK), w_scale_raw[:].rearrange("p (m t) -> p t m", t=PACK)
         )
         deal_words(nc, wc_codes[:], wc_raw[:])
-        q_sb = keep.tile([P, 2, PACK, HALF], F32, name="q_sb")
+        q_sb = keep.tile([P, J // HALF, PACK, HALF], F32, name="q_sb")
         for t in range(PACK):
             cols = slice(t * P, (t + 1) * P)
             q_psum = psum_q.tile([P, J], F32, name="q_psum")
@@ -137,57 +145,59 @@ def tile_list_expert_gated_inputs_pl_kernel(
                 start=True,
                 stop=True,
             )
-            nc.scalar.copy(q_sb[:, :, t, :], q_psum[:].rearrange("p (h j) -> p h j", h=2))
+            nc.scalar.copy(q_sb[:, :, t, :], q_psum[:].rearrange("p (h j) -> p h j", j=HALF))
 
-        t = PACK - 1
-        nc.vector.tensor_tensor(xs0[:, t, :], planes[0][t][:].indirect(offsets[:]), factor[0][t][:], ALU.mult)
+        gather_pass0(PACK - 1)
         interleave(nc.scalar.copy, xs0_bf[:], xs0[:])
         nc.vector.quantize_mx(
             out=xs0_codes[:].bitcast(FP8X4), scales=xs0_scale[:], in_=xs0_bf[:].rearrange("p j t -> p (j t)")
         )
 
-        xs1_lo = keep.tile([P, 2, J], F32, name="xs1_lo")
-        xs1_hi = [keep.tile([P, 2, SLICE], F32, name=f"xs1_hi_{s}") for s in range(SLICES)]
+        xs1_lo = keep.tile([P, PAIR, J], F32, name="xs1_lo")
+        xs1_hi = [keep.tile([P, PAIR, SLICE], F32, name=f"xs1_hi_{s}") for s in range(SLICES)]
         xs1_bf = keep.tile([P, J, PACK], BF16, name="xs1_bf", align_bytes=64)
 
         def gather_hi(t, s):
             nc.vector.tensor_tensor(
-                xs1_hi[s][:, t - 2, :],
-                planes[1][t][:].indirect(offsets[:, s * OFF_COLS : (s + 1) * OFF_COLS]),
+                xs1_hi[s][:, t - PAIR, :],
+                xf_tiles[1][t][:].indirect(offsets[:, s * LIST_COLS : (s + 1) * LIST_COLS]),
                 factor[1][t][:, s * SLICE : (s + 1) * SLICE],
                 ALU.mult,
             )
 
-        for t in range(2):
-            nc.vector.tensor_tensor(xs1_lo[:, t, :], planes[1][t][:].indirect(offsets[:]), factor[1][t][:], ALU.mult)
-        nc.scalar.copy(xs1_bf[:, :, 0:2], xs1_lo[:].rearrange("p t j -> p j t"))
+        for t in range(PAIR):
+            nc.vector.tensor_tensor(xs1_lo[:, t, :], xf_tiles[1][t][:].indirect(offsets[:]), factor[1][t][:], ALU.mult)
+        nc.scalar.copy(xs1_bf[:, :, 0:PAIR], xs1_lo[:].rearrange("p t j -> p j t"))
         for s in range(SLICES):
-            gather_hi(2, s)
+            gather_hi(PAIR, s)
 
         wa_codes = [
             keep.tile([P, N], U32, name="wa_codes_0", tag="factor_1_1", align_bytes=64),
             keep.tile([P, N], U32, name="wa_codes_1", align_bytes=64),
         ]
         for a in range(PASSES):
-            deal_words(nc, wa_codes[a][:], wa_raw[:, a, :])
+            deal_words(nc, wa_codes[a][:], wa_raw[a][:])
 
-        p_psum = [[psum.tile([P, 2, HALF], F32, name=f"p_psum_{h}_{u}") for u in range(2)] for h in range(2)]
+        p_psum = [
+            [psum.tile([P, PAIR, HALF], F32, name=f"p_psum_{h}_{u}") for u in range(PACK // PAIR)]
+            for h in range(J // HALF)
+        ]
 
         def product(a, j0, width, codes, scale):
             h, c0 = divmod(j0, HALF)
             for t in range(PACK):
                 cols = slice(t * P, (t + 1) * P)
                 nc.tensor.matmul_mx(
-                    out=p_psum[h][t // 2][:, t % 2, c0 : c0 + width],
+                    out=p_psum[h][t // PAIR][:, t % PAIR, c0 : c0 + width],
                     lhsT=wa_codes[a][:, cols].bitcast(FP8X4),
-                    lhsT_scale=w_scale[4 * (a + 1) : P, cols],
+                    lhsT_scale=w_scale[SCALE_ROWS * (a + 1) : P, cols],
                     rhs=codes.bitcast(FP8X4),
                     rhs_scale=scale,
-                    start=(a == 0 and t % 2 == 0),
-                    stop=(a == PASSES - 1 and c0 + width == HALF and t % 2 == 1),
+                    start=(a == 0 and t % PAIR == 0),
+                    stop=(a == PASSES - 1 and c0 + width == HALF and t % PAIR == PAIR - 1),
                 )
 
-        for h in range(2):
+        for h in range(J // HALF):
             js = slice(h * HALF, (h + 1) * HALF)
             product(0, h * HALF, HALF, xs0_codes[:, js], xs0_scale[:, js])
 
@@ -195,20 +205,20 @@ def tile_list_expert_gated_inputs_pl_kernel(
         y_words = out_1[0].rearrange("p c r -> p (c r)").bitcast(I32)
         y_scale = keep.tile([P, J], U8, name="y_scale", align_bytes=64)
         y_codes = keep.tile([P, J], U32, name="y_codes", align_bytes=64)
-        y = [keep.tile([P, PACK, HALF], F32, name=f"y_{h}") for h in range(2)]
+        y = [keep.tile([P, PACK, HALF], F32, name=f"y_{h}") for h in range(J // HALF)]
 
-        def front(s):
+        def finish_product(s):
             js = slice(s * SLICE, (s + 1) * SLICE)
             xs1_codes = keep.tile([P, SLICE], U32, name=f"xs1_codes_{s}", align_bytes=64)
             xs1_scale = keep.tile([P, SLICE], U8, name=f"xs1_scale_{s}", align_bytes=64)
-            nc.scalar.copy(xs1_bf[:, js, 2:4], xs1_hi[s][:].rearrange("p t j -> p j t"))
+            nc.scalar.copy(xs1_bf[:, js, PAIR:PACK], xs1_hi[s][:].rearrange("p t j -> p j t"))
             nc.vector.quantize_mx(
                 out=xs1_codes[:].bitcast(FP8X4), scales=xs1_scale[:], in_=xs1_bf[:, js, :].rearrange("p j t -> p (j t)")
             )
             product(1, s * SLICE, SLICE, xs1_codes[:], xs1_scale[:])
 
-        def result(h, u):
-            ts = slice(2 * u, 2 * u + 2)
+        def store_result(h, u):
+            ts = slice(PAIR * u, PAIR * (u + 1))
             nc.vector.scalar_tensor_tensor(
                 y[h][:, ts, :].rearrange("p t j -> p (t j)"),
                 p_psum[h][u][:].rearrange("p t j -> p (t j)"),
@@ -219,7 +229,7 @@ def tile_list_expert_gated_inputs_pl_kernel(
             )
             nc.sync.dma_start(y_rows[:, ts, h * HALF : (h + 1) * HALF], y[h][:, ts, :])
 
-        def planes_out(copy, j0, width):
+        def quantise_result(copy, j0, width):
             h, c0 = divmod(j0, HALF)
             js = slice(j0, j0 + width)
             y_bf = keep.tile([P, width, PACK], BF16, name=f"y_bf_{j0}", align_bytes=64)
@@ -229,17 +239,20 @@ def tile_list_expert_gated_inputs_pl_kernel(
             )
 
         for s in range(SLICES):
-            gather_hi(3, s)
+            gather_hi(PACK - 1, s)
         for s in range(SLICES):
-            front(s)
-        for h in range(2):
-            for u in range(2):
-                result(h, u)
-        planes_out(nc.scalar.copy, 0, HALF)
+            finish_product(s)
+        for h in range(J // HALF):
+            for u in range(PACK // PAIR):
+                store_result(h, u)
+        quantise_result(nc.scalar.copy, 0, HALF)
         nc.sync.dma_start(y_words[:, 0:HALF], y_codes[:, 0:HALF].bitcast(I32))
-        planes_out(nc.vector.tensor_copy, HALF + SLICE, SLICE)
-        planes_out(nc.scalar.copy, HALF, SLICE)
+        quantise_result(nc.vector.tensor_copy, HALF + SLICE, SLICE)
+        quantise_result(nc.scalar.copy, HALF, SLICE)
         nc.sync.dma_start(y_words[:, HALF:J], y_codes[:, HALF:J].bitcast(I32))
-        for q in range(QUADS):
-            queue = nc.scalar if q % 2 == 0 else nc.sync
-            queue.dma_start(out_2[0, 4 * q : 4 * q + 4, :].bitcast(I32), y_scale[32 * q : 32 * q + 4, :].bitcast(I32))
+        for quad in range(QUADS):
+            queue = nc.scalar if quad % 2 == 0 else nc.sync
+            queue.dma_start(
+                out_2[0, SCALE_ROWS * quad : SCALE_ROWS * (quad + 1), :].bitcast(I32),
+                y_scale[32 * quad : 32 * quad + SCALE_ROWS, :].bitcast(I32),
+            )

from contextlib import ExitStack

import concourse.mybir as mybir
from concourse.masks import make_identity

K, T, J, L, N = 1024, 2048, 512, 512, 512
FLOPS = 2 * (K + L) * N * J

F32 = mybir.dt.float32
BF16 = mybir.dt.bfloat16
I32 = mybir.dt.int32
U32 = mybir.dt.uint32
U16 = mybir.dt.uint16
U8 = mybir.dt.uint8
FP8X4 = mybir.dt.float8_e4m3fn_x4
FP4X4 = mybir.dt.float4_e2m1fn_x4
ALU = mybir.AluOpType
COPY = mybir.ActivationFunctionType.Copy

P = 128
PACK = 4
PAIR = 2
PASSES = K // (P * PACK)
QUADS = 4
SCALE_ROWS = 4
LINE = 4
SLICE = 128
SLICES = J // SLICE
LIST_COLS = SLICE // 16
HALF = J // 2


def interleave(copy, dst, src):
    copy(
        dst.rearrange("p (c i) t -> p c t i", i=LINE),
        src.rearrange("p t (c i) -> p c t i", i=LINE),
    )


def deal_words(nc, dst, src):
    nc.vector.tensor_copy(
        dst.bitcast(I32).rearrange("p (t c i) -> p c t i", t=PACK, i=LINE),
        src.rearrange("p (c i t) -> p c t i", t=PACK, i=LINE),
    )


def load_scale_rows(queue, tile, first_row, scales, quad):
    rows = scales.shape[0] * SCALE_ROWS
    queue.dma_start(
        tile[32 * quad + first_row : 32 * quad + first_row + rows, :].bitcast(I32),
        scales[:, SCALE_ROWS * quad : SCALE_ROWS * (quad + 1), :].bitcast(I32),
    )


def tile_list_expert_gated_inputs_pl_kernel(
    tc, xf, ga, fk, wa_words, wa_scales, cx_words, cx_scales, wc_words, wc_scales, offs, out_0, out_1, out_2
):
    nc = tc.nc
    with ExitStack() as ctx:
        keep = ctx.enter_context(tc.tile_pool(name="keep", bufs=1))
        psum = ctx.enter_context(tc.psum_pool(name="psum", bufs=1))
        psum_q = ctx.enter_context(tc.psum_pool(name="psum_q", bufs=2))

        xf_rows = xf.rearrange("(a p t) c -> a t p c", a=PASSES, t=PACK)
        xf_tiles = [[keep.tile([P, T], F32, name=f"xf_{a}_{t}") for t in range(PACK)] for a in range(PASSES)]
        offsets = keep.tile([P, J // 16], U16, name="offsets")
        ga_cols = keep.tile([P, PACK], F32, name="ga_cols")
        fk_cols = keep.tile([P, PASSES, 2 * PACK], F32, name="fk_cols")
        wc_raw = keep.tile([P, N], I32, name="wc_raw")
        wa_raw = [keep.tile([P, N], I32, name=f"wa_raw_{a}") for a in range(PASSES)]
        cx_codes = keep.tile([P, 2 * J], U8, name="cx_codes", align_bytes=64)
        w_scale_raw = keep.tile([P, N], U8, name="w_scale_raw")
        cx_scale = keep.tile([P, J], U8, name="cx_scale", align_bytes=64)
        ident = keep.tile([P, P], F32, name="ident")

        make_identity(nc, ident[:])
        nc.vector.memset(w_scale_raw[:].bitcast(I32), 0)
        nc.vector.memset(cx_scale[:].bitcast(I32), 0)

        nc.sync.dma_start(wc_raw[:], wc_words[0].rearrange("p n t -> p (n t)").bitcast(I32))
        nc.sync.dma_start(ga_cols[:], ga.rearrange("o (p c) -> (o p) c", c=PACK))
        nc.sync.dma_start(fk_cols[:, :, 0:PACK], fk.rearrange("(a p t) o -> p a (t o)", a=PASSES, t=PACK))
        nc.sync.dma_start(offsets[:], offs)
        nc.sync.dma_start(xf_tiles[0][0][:], xf_rows[0, 0])
        nc.sync.dma_start(xf_tiles[0][1][:], xf_rows[0, 1])
        for quad in range(QUADS // 2):
            load_scale_rows(nc.sync, w_scale_raw, 0, wc_scales, quad)
        nc.sync.dma_start(xf_tiles[0][2][:], xf_rows[0, 2])
        for quad in range(QUADS // 2, QUADS):
            load_scale_rows(nc.sync, w_scale_raw, 0, wc_scales, quad)
        nc.sync.dma_start(cx_codes[:].bitcast(I32), cx_words[0].bitcast(I32))
        nc.sync.dma_start(xf_tiles[0][3][:], xf_rows[0, 3])
        nc.sync.dma_start(wa_raw[0][:], wa_words[0].rearrange("p n t -> p (n t)").bitcast(I32))
        for quad in range(QUADS):
            load_scale_rows(nc.sync, w_scale_raw, SCALE_ROWS, wa_scales, quad)
        for t in range(PACK):
            nc.sync.dma_start(xf_tiles[1][t][:], xf_rows[1, t])
        nc.sync.dma_start(wa_raw[1][:], wa_words[1].rearrange("p n t -> p (n t)").bitcast(I32))
        for quad in range(QUADS):
            load_scale_rows(nc.gpsimd, cx_scale, 0, cx_scales, quad)

        ga_psum = psum.tile([P, PACK, P], F32, name="ga_psum")
        for c in range(PACK):
            nc.tensor.transpose(ga_psum[:, c, :], ga_cols[:, c : c + 1].to_broadcast([P, P]), ident[:])
        factor = [
            [keep.tile([P, J], F32, name=f"factor_{a}_{t}", tag=f"factor_{a}_{t}", align_bytes=64) for t in range(PACK)]
            for a in range(PASSES)
        ]
        for a in range(PASSES):
            for t in range(PACK):
                nc.scalar.activation(
                    factor[a][t][:].rearrange("p (n c) -> p n c", c=PACK),
                    ga_psum[:].rearrange("p c n -> p n c"),
                    COPY,
                    scale=fk_cols[:, a, t : t + 1],
                )

        xs0 = keep.tile([P, PACK, J], F32, name="xs0")
        xs0_bf = keep.tile([P, J, PACK], BF16, name="xs0_bf", align_bytes=64)
        xs0_codes = keep.tile([P, J], U32, name="xs0_codes", align_bytes=64)
        xs0_scale = keep.tile([P, J], U8, name="xs0_scale", align_bytes=64)

        def gather_pass0(t):
            nc.vector.tensor_tensor(xs0[:, t, :], xf_tiles[0][t][:].indirect(offsets[:]), factor[0][t][:], ALU.mult)

        for t in range(PACK - 1):
            gather_pass0(t)

        w_scale = keep.tile([P, N], U8, name="w_scale", align_bytes=64)
        wc_codes = keep.tile([P, N], U32, name="wc_codes", align_bytes=64)
        nc.vector.tensor_copy(
            w_scale[:].rearrange("p (t m) -> p t m", t=PACK), w_scale_raw[:].rearrange("p (m t) -> p t m", t=PACK)
        )
        deal_words(nc, wc_codes[:], wc_raw[:])
        q_sb = keep.tile([P, J // HALF, PACK, HALF], F32, name="q_sb")
        for t in range(PACK):
            cols = slice(t * P, (t + 1) * P)
            q_psum = psum_q.tile([P, J], F32, name="q_psum")
            nc.tensor.matmul_mx(
                out=q_psum[:],
                lhsT=wc_codes[:, cols].bitcast(FP8X4),
                lhsT_scale=w_scale[:, cols],
                rhs=cx_codes[:].bitcast(FP4X4),
                rhs_scale=cx_scale[:],
                start=True,
                stop=True,
            )
            nc.scalar.copy(q_sb[:, :, t, :], q_psum[:].rearrange("p (h j) -> p h j", j=HALF))

        gather_pass0(PACK - 1)
        interleave(nc.scalar.copy, xs0_bf[:], xs0[:])
        nc.vector.quantize_mx(
            out=xs0_codes[:].bitcast(FP8X4), scales=xs0_scale[:], in_=xs0_bf[:].rearrange("p j t -> p (j t)")
        )

        xs1_lo = keep.tile([P, PAIR, J], F32, name="xs1_lo")
        xs1_hi = [keep.tile([P, PAIR, SLICE], F32, name=f"xs1_hi_{s}") for s in range(SLICES)]
        xs1_bf = keep.tile([P, J, PACK], BF16, name="xs1_bf", align_bytes=64)

        def gather_hi(t, s):
            nc.vector.tensor_tensor(
                xs1_hi[s][:, t - PAIR, :],
                xf_tiles[1][t][:].indirect(offsets[:, s * LIST_COLS : (s + 1) * LIST_COLS]),
                factor[1][t][:, s * SLICE : (s + 1) * SLICE],
                ALU.mult,
            )

        for t in range(PAIR):
            nc.vector.tensor_tensor(xs1_lo[:, t, :], xf_tiles[1][t][:].indirect(offsets[:]), factor[1][t][:], ALU.mult)
        nc.scalar.copy(xs1_bf[:, :, 0:PAIR], xs1_lo[:].rearrange("p t j -> p j t"))
        for s in range(SLICES):
            gather_hi(PAIR, s)

        wa_codes = [
            keep.tile([P, N], U32, name="wa_codes_0", tag="factor_1_1", align_bytes=64),
            keep.tile([P, N], U32, name="wa_codes_1", align_bytes=64),
        ]
        for a in range(PASSES):
            deal_words(nc, wa_codes[a][:], wa_raw[a][:])

        p_psum = [
            [psum.tile([P, PAIR, HALF], F32, name=f"p_psum_{h}_{u}") for u in range(PACK // PAIR)]
            for h in range(J // HALF)
        ]

        def product(a, j0, width, codes, scale):
            h, c0 = divmod(j0, HALF)
            for t in range(PACK):
                cols = slice(t * P, (t + 1) * P)
                nc.tensor.matmul_mx(
                    out=p_psum[h][t // PAIR][:, t % PAIR, c0 : c0 + width],
                    lhsT=wa_codes[a][:, cols].bitcast(FP8X4),
                    lhsT_scale=w_scale[SCALE_ROWS * (a + 1) : P, cols],
                    rhs=codes.bitcast(FP8X4),
                    rhs_scale=scale,
                    start=(a == 0 and t % PAIR == 0),
                    stop=(a == PASSES - 1 and c0 + width == HALF and t % PAIR == PAIR - 1),
                )

        for h in range(J // HALF):
            js = slice(h * HALF, (h + 1) * HALF)
            product(0, h * HALF, HALF, xs0_codes[:, js], xs0_scale[:, js])

        y_rows = out_0.rearrange("(p t) j -> p t j", t=PACK)
        y_words = out_1[0].rearrange("p c r -> p (c r)").bitcast(I32)
        y_scale = keep.tile([P, J], U8, name="y_scale", align_bytes=64)
        y_codes = keep.tile([P, J], U32, name="y_codes", align_bytes=64)
        y = [keep.tile([P, PACK, HALF], F32, name=f"y_{h}") for h in range(J // HALF)]

        def finish_product(s):
            js = slice(s * SLICE, (s + 1) * SLICE)
            xs1_codes = keep.tile([P, SLICE], U32, name=f"xs1_codes_{s}", align_bytes=64)
            xs1_scale = keep.tile([P, SLICE], U8, name=f"xs1_scale_{s}", align_bytes=64)
            nc.scalar.copy(xs1_bf[:, js, PAIR:PACK], xs1_hi[s][:].rearrange("p t j -> p j t"))
            nc.vector.quantize_mx(
                out=xs1_codes[:].bitcast(FP8X4), scales=xs1_scale[:], in_=xs1_bf[:, js, :].rearrange("p j t -> p (j t)")
            )
            product(1, s * SLICE, SLICE, xs1_codes[:], xs1_scale[:])

        def store_result(h, u):
            ts = slice(PAIR * u, PAIR * (u + 1))
            nc.vector.scalar_tensor_tensor(
                y[h][:, ts, :].rearrange("p t j -> p (t j)"),
                p_psum[h][u][:].rearrange("p t j -> p (t j)"),
                0.0,
                q_sb[:, h, ts, :].rearrange("p t j -> p (t j)"),
                ALU.max,
                ALU.add,
            )
            nc.sync.dma_start(y_rows[:, ts, h * HALF : (h + 1) * HALF], y[h][:, ts, :])

        def quantise_result(copy, j0, width):
            h, c0 = divmod(j0, HALF)
            js = slice(j0, j0 + width)
            y_bf = keep.tile([P, width, PACK], BF16, name=f"y_bf_{j0}", align_bytes=64)
            interleave(copy, y_bf[:], y[h][:, :, c0 : c0 + width])
            nc.vector.quantize_mx(
                out=y_codes[:, js].bitcast(FP8X4), scales=y_scale[:, js], in_=y_bf[:].rearrange("p j t -> p (j t)")
            )

        for s in range(SLICES):
            gather_hi(PACK - 1, s)
        for s in range(SLICES):
            finish_product(s)
        for h in range(J // HALF):
            for u in range(PACK // PAIR):
                store_result(h, u)
        quantise_result(nc.scalar.copy, 0, HALF)
        nc.sync.dma_start(y_words[:, 0:HALF], y_codes[:, 0:HALF].bitcast(I32))
        quantise_result(nc.vector.tensor_copy, HALF + SLICE, SLICE)
        quantise_result(nc.scalar.copy, HALF, SLICE)
        nc.sync.dma_start(y_words[:, HALF:J], y_codes[:, HALF:J].bitcast(I32))
        for quad in range(QUADS):
            queue = nc.scalar if quad % 2 == 0 else nc.sync
            queue.dma_start(
                out_2[0, SCALE_ROWS * quad : SCALE_ROWS * (quad + 1), :].bitcast(I32),
                y_scale[32 * quad : 32 * quad + SCALE_ROWS, :].bitcast(I32),
            )
